import numpy as np
import ml_dtypes


def mxq(x, axis, fmt="e4m3"):
    dtype, down = {"e4m3": (ml_dtypes.float8_e4m3fn, 7), "e5m2": (ml_dtypes.float8_e5m2, 14)}[fmt]
    v = np.moveaxis(np.asarray(x, np.float32).astype(ml_dtypes.bfloat16).astype(np.float64), axis, -1)
    blocks = v.reshape(v.shape[:-1] + (-1, 32))
    amax = np.abs(blocks).max(-1, keepdims=True)
    byte = np.maximum(np.where(amax > 0, np.frexp(amax)[1] - 1 + 127, 0) - down, 1)
    scale = np.exp2(byte - 127.0)
    codes = (blocks / scale).astype(np.float32).astype(dtype).astype(np.float64)
    return np.moveaxis((codes * scale).reshape(v.shape), -1, axis)


WIDE = False


def mx_kscale(k):
    if not WIDE:
        return np.ones(k)
    levels = np.array([10, -10, 5, -5, 0])
    if k % 512:
        return np.exp2(np.random.permutation(np.resize(levels, k // 32))).repeat(32)
    a = np.empty((k // 512, 16))
    for p in range(k // 512):
        a[p, :8] = np.random.permutation(np.resize(levels, 8))
        for g in range(8):
            far = levels[np.abs(levels - a[p, g]) >= 10]
            a[p, g + 8] = far[np.random.randint(len(far))]
    return np.exp2(a.ravel()).repeat(32)


def f64(x):
    return np.asarray(x).astype(np.float64)


def striped(idx):
    return np.tile(idx.reshape(-1, 16).T, (8, 1)).astype(np.uint16)


def unstriped(offs):
    return offs[:16].T.reshape(-1).astype(np.int64)


def striped8(idx):
    return np.concatenate([x.reshape(-1, 16).T for x in idx]).astype(np.uint16)


def runs(offs, k):
    lists = np.stack([offs[16 * r : 16 * r + 16].T.reshape(-1) for r in range(8)]).astype(np.int64)
    return lists[np.arange(k) % 512 // 64]


def pack_weight(w):
    k, n = w.shape
    w = f64(np.asarray(w, np.float32).astype(ml_dtypes.bfloat16)).reshape(k // 32, 32, n)
    amax = np.abs(w).max(1)
    byte = np.clip(np.where(amax > 0, np.frexp(amax)[1] - 1 + 127 - 7, 1), 1, 254)
    scaled = (w * np.exp2(127.0 - byte)[:, None, :]).reshape(k, n).astype(np.float32)
    words = np.ascontiguousarray(scaled.reshape(k // 512, 128, 4, n).transpose(0, 1, 3, 2)).astype(ml_dtypes.float8_e4m3fn).view(np.uint8)
    return words, np.ascontiguousarray(byte.astype(np.uint8).reshape(k // 512, 16, n))


def unpack_weight(words, scales):
    g, p, n, _ = words.shape
    vals = np.ascontiguousarray(words).view(ml_dtypes.float8_e4m3fn).astype(np.float64) * np.repeat(np.exp2(scales.astype(np.float64) - 127.0), 8, axis=1)[..., None]
    return vals.transpose(0, 1, 3, 2).reshape(g * 512, n)


def sigmoid(v):
    return 1.0 / (1.0 + np.exp(-np.maximum(v, -700.0)))


K, T, S, H, W, C = 512, 2048, 256, 512, 128, 512


def setup_inputs():
    n = np.random.standard_normal
    s = mx_kscale(K)[:, None]
    packed_xT = pack_weight(n((K, T)) * s)
    perm = np.random.permutation(S)
    return {
        "x_words": packed_xT[0],
        "x_scales": packed_xT[1],
        "w1": (n((K, H)) / np.sqrt(K) / s).astype(np.float32),
        "gs": (np.random.uniform(0.5, 1.5, (K, 1)) / s).astype(np.float32),
        "offs": striped8(np.random.randint(0, T, (8, S))),
        "n1": striped(perm[:W]),
        "n2": striped(perm[W:]),
        "cand": striped8(np.random.randint(0, T, (8, C))),
        "n3": striped8(np.stack([np.random.permutation(S) for _ in range(8)])),
        "n4": striped8(np.stack([np.random.permutation(S) for _ in range(8)])),
    }


def reference(x_words, x_scales, w1, gs, offs, n1, n2, cand, n3, n4):
    x_cand = unpack_weight(x_words, x_scales)[np.arange(K)[:, None], runs(cand, K)]
    xq = unpack_weight(x_words, x_scales)[np.arange(K)[:, None], runs(offs, K)]
    y = mxq(f64(w1), 0, "e4m3").T @ xq
    pa = y[:, unstriped(n1)]
    pb = y[:, unstriped(n2)]
    rb = np.minimum(pa, pb)
    ra = np.maximum(pa, pb)
    ds = np.zeros((H, S))
    ds[:, unstriped(n1)] = ra
    dt = ds.copy()
    dt[:, unstriped(n2)] = rb
    z = f64(gs) * dt
    s = 0.0625 * ((x_cand.T @ mxq(z, 0, "e4m3")))
    return (s - (s[np.arange(C)[:, None], runs(n3, C)])) * (sigmoid(s[np.arange(C)[:, None], runs(n4, C)]))

@@ -1,0 +1,164 @@
+from contextlib import ExitStack
+
+import concourse.mybir as mybir
+
+F32 = mybir.dt.float32
+BF16 = mybir.dt.bfloat16
+I32 = mybir.dt.int32
+U32 = mybir.dt.uint32
+U16 = mybir.dt.uint16
+U8 = mybir.dt.uint8
+FP8X4 = mybir.dt.float8_e4m3fn_x4
+ALU = mybir.AluOpType
+ACT = mybir.ActivationFunctionType
+
+P = 128
+PACK = 4
+K, T, S, H, W, C = 512, 2048, 256, 512, 128, 512
+FLOPS = 2 * K * H * S + 2 * K * C * S
+M_SPLIT = 80
+
+
+def tile_picked_hcandordergdif_none_p_kernel(
+    tc, x_words, x_scales, w1, gs, offs, n1, n2, cand, n3, n4, out
+):
+    nc = tc.nc
+    with ExitStack() as ctx:
+        keep = ctx.enter_context(tc.tile_pool(name="keep", bufs=1))
+        psum = ctx.enter_context(tc.psum_pool(name="psum", bufs=1))
+
+        def load_list(src, name):
+            tile = keep.tile(list(src.shape), U16, name=name)
+            nc.sync.dma_start(tile[:], src)
+            return tile
+
+        scale_table = keep.tile([P, T], U8, name="scale_table")
+        nc.vector.memset(scale_table[:].bitcast(I32), 0)
+        scale_rows = x_scales[0].rearrange("(r e) c -> e r c", e=2)
+        for e in range(2):
+            nc.scalar.dma_start(scale_table[e:P:16, :].bitcast(I32), scale_rows[e].bitcast(I32))
+
+        offs_t = load_list(offs, "offs_t")
+        w_raw = keep.tile([P, PACK, H], F32, name="w_raw")
+        nc.sync.dma_start(w_raw[:], w1.rearrange("(p j) c -> p j c", j=PACK))
+        word_table = keep.tile([P, T], U32, name="word_table")
+        nc.sync.dma_start(word_table[:].bitcast(I32), x_words[0].rearrange("p c r -> p (c r)").bitcast(I32))
+        cand_t = load_list(cand, "cand_t")
+        n1_t = load_list(n1, "n1_t")
+        n2_t = load_list(n2, "n2_t")
+        n3_t = load_list(n3, "n3_t")
+        n4_t = load_list(n4, "n4_t")
+        gs_t = keep.tile([P, PACK], F32, name="gs_t")
+        nc.gpsimd.dma_start(gs_t[:], gs.rearrange("(p t) o -> p (t o)", t=PACK))
+
+        def scale_plane(picked, width, name, queue):
+            plane = keep.tile([P, width], U8, name=name, align_bytes=64)
+            nc.vector.tensor_copy(plane[:].bitcast(I32), picked[:].bitcast(I32))
+            for e in range(2):
+                queue.dma_start(plane[2 + e : P : 32, :].bitcast(I32), picked[16 + e : P : 32, :].bitcast(I32))
+            return plane
+
+        place_bytes = keep.tile([P, S], U8, name="place_bytes")
+        nc.vector.tensor_copy(place_bytes[:], scale_table[:].indirect(offs_t[:]))
+        place_plane = scale_plane(place_bytes, S, "place_plane", nc.scalar)
+
+        w_bf = keep.tile([P, PACK * H], BF16, name="w_bf", align_bytes=64)
+        w_dst = w_bf[:].rearrange("p (t m j) -> p m j t", t=PACK, j=PACK)
+        w_src = w_raw[:].rearrange("p j (m t) -> p m j t", t=PACK)
+        nc.vector.tensor_copy(w_dst[:, :M_SPLIT], w_src[:, :M_SPLIT])
+        nc.scalar.copy(w_dst[:, M_SPLIT:], w_src[:, M_SPLIT:])
+        w_codes = keep.tile([P, H], U32, name="w_codes", align_bytes=64)
+        w_plane = keep.tile([P, H], U8, name="w_plane", align_bytes=64)
+        nc.vector.quantize_mx(out=w_codes[:].bitcast(FP8X4), scales=w_plane[:], in_=w_bf[:])
+
+        place_words = keep.tile([P, S], U32, name="place_words", tag="picked_words", align_bytes=64)
+        nc.vector.tensor_copy(place_words[:], word_table[:].indirect(offs_t[:]))
+
+        rows = [keep.tile([P, 2 * S], F32, name="rows%d" % t) for t in range(PACK)]
+        for t in range(PACK):
+            cols = slice(t * P, (t + 1) * P)
+            y_bank = psum.tile([P, S], F32, name="y_bank%d" % t)
+            nc.tensor.matmul_mx(
+                out=y_bank[:], lhsT=w_codes[:, cols].bitcast(FP8X4), lhsT_scale=w_plane[:, cols],
+                rhs=place_words[:].bitcast(FP8X4), rhs_scale=place_plane[:], start=True, stop=True,
+            )
+            if t == 0:
+                nc.scalar.copy(rows[t][:, S:], y_bank[:])
+            else:
+                nc.vector.tensor_copy(rows[t][:, S:], y_bank[:])
+
+        pair = [[keep.tile([P, W], F32, name="pair%d_%d" % (t, u)) for u in range(2)] for t in range(PACK)]
+        sort = [[keep.tile([P, W], F32, name="sort%d_%d" % (t, u)) for u in range(2)] for t in range(PACK)]
+        placed = [keep.tile([P, S], F32, name="placed%d" % t) for t in range(PACK)]
+        z_bf = [keep.tile([P, S // 2, PACK], BF16, name="z_bf%d" % h, align_bytes=64) for h in range(2)]
+        pair_lists = (n1_t, n2_t)
+
+        def fetch(t, u):
+            nc.scalar.activation(pair[t][u][:], rows[t][:, S:].indirect(pair_lists[u][:]), ACT.Copy)
+            if u == 1:
+                nc.vector.tensor_tensor(sort[t][0][:], pair[t][0][:], pair[t][1][:], ALU.max)
+                nc.vector.tensor_tensor(sort[t][1][:], pair[t][0][:], pair[t][1][:], ALU.min)
+
+        def put(t, u):
+            nc.scalar.activation(placed[t][:].indirect(pair_lists[u][:]), sort[t][u][:], ACT.Copy)
+            if u == 1:
+                for h in range(2):
+                    nc.vector.tensor_scalar(
+                        z_bf[h][:, :, t], placed[t][:, h * W : (h + 1) * W], gs_t[:, t : t + 1], None, ALU.mult
+                    )
+
+        fetch(0, 0)
+        fetch(0, 1)
+        fetch(1, 0)
+        fetch(1, 1)
+        for t in range(2):
+            for u in range(2):
+                put(t, u)
+                fetch(t + 2, u)
+        for u in range(2):
+            put(2, u)
+            put(3, u)
+
+        cand_bytes = keep.tile([P, C], U8, name="cand_bytes")
+        nc.vector.tensor_copy(cand_bytes[:], scale_table[:].indirect(cand_t[:]))
+        dealt_bytes = keep.tile([P, C], U8, name="dealt_bytes")
+        nc.vector.tensor_copy(
+            dealt_bytes[:].rearrange("p (t m) -> p m t", t=PACK), cand_bytes[:].rearrange("p (m t) -> p m t", t=PACK)
+        )
+        cand_plane = scale_plane(dealt_bytes, C, "cand_plane", nc.sync)
+        cand_words = keep.tile([P, C], U32, name="cand_words", tag="picked_words", align_bytes=64)
+        nc.vector.tensor_copy(cand_words[:], word_table[:].indirect(cand_t[:]))
+        dealt_words = keep.tile([P, C], U32, name="dealt_words", align_bytes=64)
+        nc.vector.tensor_copy(
+            dealt_words[:].bitcast(I32).rearrange("p (t m) -> p m t", t=PACK),
+            cand_words[:].bitcast(I32).rearrange("p (m t) -> p m t", t=PACK),
+        )
+
+        z_codes = keep.tile([P, S], U32, name="z_codes", align_bytes=64)
+        z_plane = keep.tile([P, S], U8, name="z_plane", align_bytes=64)
+        for h in range(2):
+            half = slice(h * W, (h + 1) * W)
+            nc.vector.quantize_mx(
+                out=z_codes[:, half].bitcast(FP8X4), scales=z_plane[:, half],
+                in_=z_bf[h][:].rearrange("p j t -> p (j t)"),
+            )
+
+        out_rows = out.rearrange("(p t) j -> p t j", t=PACK)
+        for t in range(PACK):
+            cols = slice(t * P, (t + 1) * P)
+            s_bank = psum.tile([P, S], F32, name="s_bank%d" % t)
+            nc.tensor.matmul_mx(
+                out=s_bank[:], lhsT=dealt_words[:, cols].bitcast(FP8X4), lhsT_scale=cand_plane[:, cols],
+                rhs=z_codes[:].bitcast(FP8X4), rhs_scale=z_plane[:], start=True, stop=True,
+            )
+            nc.vector.tensor_scalar(rows[t][:, :S], s_bank[:], 0.0625, None, ALU.mult)
+        for t in range(PACK):
+            other = keep.tile([P, S], F32, name="other%d" % t)
+            gate = keep.tile([P, S], F32, name="gate%d" % t)
+            diff = keep.tile([P, S], F32, name="diff%d" % t)
+            result = keep.tile([P, S], F32, name="result%d" % t)
+            nc.scalar.activation(other[:], rows[t][:].indirect(n3_t[:]), ACT.Copy)
+            nc.scalar.activation(gate[:], rows[t][:].indirect(n4_t[:]), ACT.Sigmoid)
+            nc.vector.tensor_tensor(diff[:], rows[t][:, :S], other[:], ALU.subtract)
+            nc.vector.tensor_tensor(result[:], diff[:], gate[:], ALU.mult)
+            nc.sync.dma_start(out_rows[:, t, :], result[:])

@@ -33,34 +33,36 @@ def tile_picked_hcandordergdif_none_p_kernel(
             return tile
 
         scale_table = keep.tile([P, T], U8, name="scale_table")
-        nc.vector.memset(scale_table[:].bitcast(I32), 0)
-        scale_rows = x_scales[0].rearrange("(r e) c -> e r c", e=2)
-        for e in range(2):
-            nc.scalar.dma_start(scale_table[e:P:16, :].bitcast(I32), scale_rows[e].bitcast(I32))
-
+        nc.sync.dma_start(
+            scale_table[:].bitcast(I32), x_scales[0].bitcast(I32).unsqueeze(1).to_broadcast([16, 8, T // 4])
+        )
         offs_t = load_list(offs, "offs_t")
+        cand_t = load_list(cand, "cand_t")
+        n1_t = load_list(n1, "n1_t")
         w_raw = keep.tile([P, PACK, H], F32, name="w_raw")
         nc.sync.dma_start(w_raw[:], w1.rearrange("(p j) c -> p j c", j=PACK))
         word_table = keep.tile([P, T], U32, name="word_table")
         nc.sync.dma_start(word_table[:].bitcast(I32), x_words[0].rearrange("p c r -> p (c r)").bitcast(I32))
-        cand_t = load_list(cand, "cand_t")
-        n1_t = load_list(n1, "n1_t")
         n2_t = load_list(n2, "n2_t")
         n3_t = load_list(n3, "n3_t")
         n4_t = load_list(n4, "n4_t")
         gs_t = keep.tile([P, PACK], F32, name="gs_t")
+
+        warm_in = keep.tile([P, 1], F32, name="warm_in")
+        warm_out = keep.tile([P, 1], F32, name="warm_out")
+        nc.gpsimd.memset(warm_in[:], 0.0)
+        nc.scalar.activation(warm_out[:], warm_in[:], ACT.Sigmoid)
         nc.gpsimd.dma_start(gs_t[:], gs.rearrange("(p t) o -> p (t o)", t=PACK))
 
-        def scale_plane(picked, width, name, queue):
-            plane = keep.tile([P, width], U8, name=name, align_bytes=64)
-            nc.vector.tensor_copy(plane[:].bitcast(I32), picked[:].bitcast(I32))
-            for e in range(2):
-                queue.dma_start(plane[2 + e : P : 32, :].bitcast(I32), picked[16 + e : P : 32, :].bitcast(I32))
-            return plane
+        def close_up_rows(plane, queue):
+            for i in range(1, 4):
+                queue.dma_start(plane[i:P:32, :].bitcast(I32), plane[8 * i : P : 32, :].bitcast(I32))
 
         place_bytes = keep.tile([P, S], U8, name="place_bytes")
         nc.vector.tensor_copy(place_bytes[:], scale_table[:].indirect(offs_t[:]))
-        place_plane = scale_plane(place_bytes, S, "place_plane", nc.scalar)
+        place_plane = keep.tile([P, S], U8, name="place_plane", align_bytes=64)
+        nc.vector.tensor_copy(place_plane[:].bitcast(I32), place_bytes[:].bitcast(I32))
+        close_up_rows(place_plane, nc.scalar)
 
         w_bf = keep.tile([P, PACK * H], BF16, name="w_bf", align_bytes=64)
         w_dst = w_bf[:].rearrange("p (t m j) -> p m j t", t=PACK, j=PACK)
@@ -75,17 +77,25 @@ def tile_picked_hcandordergdif_none_p_kernel(
         nc.vector.tensor_copy(place_words[:], word_table[:].indirect(offs_t[:]))
 
         rows = [keep.tile([P, 2 * S], F32, name="rows%d" % t) for t in range(PACK)]
-        for t in range(PACK):
+
+        def product(t, lhs_words, lhs_plane, rhs_words, rhs_plane, dst, factor):
             cols = slice(t * P, (t + 1) * P)
-            y_bank = psum.tile([P, S], F32, name="y_bank%d" % t)
-            nc.tensor.matmul_mx(
-                out=y_bank[:], lhsT=w_codes[:, cols].bitcast(FP8X4), lhsT_scale=w_plane[:, cols],
-                rhs=place_words[:].bitcast(FP8X4), rhs_scale=place_plane[:], start=True, stop=True,
-            )
-            if t == 0:
-                nc.scalar.copy(rows[t][:, S:], y_bank[:])
-            else:
-                nc.vector.tensor_copy(rows[t][:, S:], y_bank[:])
+            pieces = 2 if t == 0 else 1
+            width = S // pieces
+            for h in range(pieces):
+                part = slice(h * width, (h + 1) * width)
+                bank = psum.tile([P, width], F32, name="bank", tag="bank%d_%d" % (t, h))
+                nc.tensor.matmul_mx(
+                    out=bank[:], lhsT=lhs_words[:, cols].bitcast(FP8X4), lhsT_scale=lhs_plane[:, cols],
+                    rhs=rhs_words[:, part].bitcast(FP8X4), rhs_scale=rhs_plane[:, part], start=True, stop=True,
+                )
+                if h == 1:
+                    nc.scalar.activation(dst[:, part], bank[:], ACT.Copy, scale=factor)
+                else:
+                    nc.vector.tensor_scalar(dst[:, part], bank[:], factor, None, ALU.mult)
+
+        for t in range(PACK):
+            product(t, w_codes, w_plane, place_words, place_plane, rows[t][:, S:], 1.0)
 
         pair = [[keep.tile([P, W], F32, name="pair%d_%d" % (t, u)) for u in range(2)] for t in range(PACK)]
         sort = [[keep.tile([P, W], F32, name="sort%d_%d" % (t, u)) for u in range(2)] for t in range(PACK)]
@@ -121,11 +131,11 @@ def tile_picked_hcandordergdif_none_p_kernel(
 
         cand_bytes = keep.tile([P, C], U8, name="cand_bytes")
         nc.vector.tensor_copy(cand_bytes[:], scale_table[:].indirect(cand_t[:]))
-        dealt_bytes = keep.tile([P, C], U8, name="dealt_bytes")
+        cand_plane = keep.tile([P, C], U8, name="cand_plane", align_bytes=64)
         nc.vector.tensor_copy(
-            dealt_bytes[:].rearrange("p (t m) -> p m t", t=PACK), cand_bytes[:].rearrange("p (m t) -> p m t", t=PACK)
+            cand_plane[:].rearrange("p (t m) -> p m t", t=PACK), cand_bytes[:].rearrange("p (m t) -> p m t", t=PACK)
         )
-        cand_plane = scale_plane(dealt_bytes, C, "cand_plane", nc.sync)
+        close_up_rows(cand_plane, nc.sync)
         cand_words = keep.tile([P, C], U32, name="cand_words", tag="picked_words", align_bytes=64)
         nc.vector.tensor_copy(cand_words[:], word_table[:].indirect(cand_t[:]))
         dealt_words = keep.tile([P, C], U32, name="dealt_words", align_bytes=64)
@@ -145,20 +155,19 @@ def tile_picked_hcandordergdif_none_p_kernel(
 
         out_rows = out.rearrange("(p t) j -> p t j", t=PACK)
         for t in range(PACK):
-            cols = slice(t * P, (t + 1) * P)
-            s_bank = psum.tile([P, S], F32, name="s_bank%d" % t)
-            nc.tensor.matmul_mx(
-                out=s_bank[:], lhsT=dealt_words[:, cols].bitcast(FP8X4), lhsT_scale=cand_plane[:, cols],
-                rhs=z_codes[:].bitcast(FP8X4), rhs_scale=z_plane[:], start=True, stop=True,
-            )
-            nc.vector.tensor_scalar(rows[t][:, :S], s_bank[:], 0.0625, None, ALU.mult)
+            product(t, dealt_words, cand_plane, z_codes, z_plane, rows[t][:, :S], 0.0625)
         for t in range(PACK):
             other = keep.tile([P, S], F32, name="other%d" % t)
-            gate = keep.tile([P, S], F32, name="gate%d" % t)
             diff = keep.tile([P, S], F32, name="diff%d" % t)
-            result = keep.tile([P, S], F32, name="result%d" % t)
             nc.scalar.activation(other[:], rows[t][:].indirect(n3_t[:]), ACT.Copy)
-            nc.scalar.activation(gate[:], rows[t][:].indirect(n4_t[:]), ACT.Sigmoid)
             nc.vector.tensor_tensor(diff[:], rows[t][:, :S], other[:], ALU.subtract)
-            nc.vector.tensor_tensor(result[:], diff[:], gate[:], ALU.mult)
-            nc.sync.dma_start(out_rows[:, t, :], result[:])
+            pieces = 2 if t == PACK - 1 else 1
+            width = S // pieces
+            for h in range(pieces):
+                part = slice(h * width, (h + 1) * width)
+                gate = keep.tile([P, width], F32, name="gate%d_%d" % (t, h))
+                result = keep.tile([P, width], F32, name="result%d_%d" % (t, h))
+                offsets = n4_t[:, h * width // 16 : (h + 1) * width // 16]
+                nc.scalar.activation(gate[:], rows[t][:].indirect(offsets), ACT.Sigmoid)
+                nc.vector.tensor_tensor(result[:], diff[:, part], gate[:], ALU.mult)
+                nc.sync.dma_start(out_rows[:, t, part], result[:])

@@ -133,15 +133,16 @@ def tile_picked_hcandordergdif_none_p_kernel(
         nc.vector.tensor_copy(cand_bytes[:], scale_table[:].indirect(cand_t[:]))
         cand_plane = keep.tile([P, C], U8, name="cand_plane", align_bytes=64)
         nc.vector.tensor_copy(
-            cand_plane[:].rearrange("p (t m) -> p m t", t=PACK), cand_bytes[:].rearrange("p (m t) -> p m t", t=PACK)
+            cand_plane[:].bitcast(I32).rearrange("p (t g) -> p g t", t=PACK),
+            cand_bytes[:].bitcast(I32).rearrange("p (g t) -> p g t", t=PACK),
         )
         close_up_rows(cand_plane, nc.sync)
         cand_words = keep.tile([P, C], U32, name="cand_words", tag="picked_words", align_bytes=64)
         nc.vector.tensor_copy(cand_words[:], word_table[:].indirect(cand_t[:]))
         dealt_words = keep.tile([P, C], U32, name="dealt_words", align_bytes=64)
         nc.vector.tensor_copy(
-            dealt_words[:].bitcast(I32).rearrange("p (t m) -> p m t", t=PACK),
-            cand_words[:].bitcast(I32).rearrange("p (m t) -> p m t", t=PACK),
+            dealt_words[:].bitcast(I32).rearrange("p (t g a) -> p g t a", t=PACK, a=4),
+            cand_words[:].bitcast(I32).rearrange("p (g t a) -> p g t a", t=PACK, a=4),
         )
 
         z_codes = keep.tile([P, S], U32, name="z_codes", align_bytes=64)
@@ -153,7 +154,7 @@ def tile_picked_hcandordergdif_none_p_kernel(
                 in_=z_bf[h][:].rearrange("p j t -> p (j t)"),
             )
 
-        out_rows = out.rearrange("(p t) j -> p t j", t=PACK)
+        out_rows = out.rearrange("(g t a) j -> t g a j", t=PACK, a=4)
         for t in range(PACK):
             product(t, dealt_words, cand_plane, z_codes, z_plane, rows[t][:, :S], 0.0625)
         for t in range(PACK):
@@ -170,4 +171,4 @@ def tile_picked_hcandordergdif_none_p_kernel(
                 offsets = n4_t[:, h * width // 16 : (h + 1) * width // 16]
                 nc.scalar.activation(gate[:], rows[t][:].indirect(offsets), ACT.Sigmoid)
                 nc.vector.tensor_tensor(result[:], diff[:, part], gate[:], ALU.mult)
-                nc.sync.dma_start(out_rows[:, t, part], result[:])
+                nc.sync.dma_start(out_rows[t][:, :, part], result[:])

from contextlib import ExitStack

import concourse.mybir as mybir

F32 = mybir.dt.float32
BF16 = mybir.dt.bfloat16
I32 = mybir.dt.int32
U32 = mybir.dt.uint32
U16 = mybir.dt.uint16
U8 = mybir.dt.uint8
FP8X4 = mybir.dt.float8_e4m3fn_x4
ALU = mybir.AluOpType
ACT = mybir.ActivationFunctionType

P = 128
PACK = 4
K, T, S, H, W, C = 512, 2048, 256, 512, 128, 512
FLOPS = 2 * K * H * S + 2 * K * C * S
M_SPLIT = 80


def tile_picked_hcandordergdif_none_p_kernel(
    tc, x_words, x_scales, w1, gs, offs, n1, n2, cand, n3, n4, out
):
    nc = tc.nc
    with ExitStack() as ctx:
        keep = ctx.enter_context(tc.tile_pool(name="keep", bufs=1))
        psum = ctx.enter_context(tc.psum_pool(name="psum", bufs=1))

        def load_list(src, name):
            tile = keep.tile(list(src.shape), U16, name=name)
            nc.sync.dma_start(tile[:], src)
            return tile

        scale_table = keep.tile([P, T], U8, name="scale_table")
        nc.sync.dma_start(
            scale_table[:].bitcast(I32), x_scales[0].bitcast(I32).unsqueeze(1).to_broadcast([16, 8, T // 4])
        )
        offs_t = load_list(offs, "offs_t")
        cand_t = load_list(cand, "cand_t")
        n1_t = load_list(n1, "n1_t")
        w_raw = keep.tile([P, PACK, H], F32, name="w_raw")
        nc.sync.dma_start(w_raw[:], w1.rearrange("(p j) c -> p j c", j=PACK))
        word_table = keep.tile([P, T], U32, name="word_table")
        nc.sync.dma_start(word_table[:].bitcast(I32), x_words[0].rearrange("p c r -> p (c r)").bitcast(I32))
        n2_t = load_list(n2, "n2_t")
        n3_t = load_list(n3, "n3_t")
        n4_t = load_list(n4, "n4_t")
        gs_t = keep.tile([P, PACK], F32, name="gs_t")

        warm_in = keep.tile([P, 1], F32, name="warm_in")
        warm_out = keep.tile([P, 1], F32, name="warm_out")
        nc.gpsimd.memset(warm_in[:], 0.0)
        nc.scalar.activation(warm_out[:], warm_in[:], ACT.Sigmoid)
        nc.gpsimd.dma_start(gs_t[:], gs.rearrange("(p t) o -> p (t o)", t=PACK))

        def close_up_rows(plane, queue):
            for i in range(1, 4):
                queue.dma_start(plane[i:P:32, :].bitcast(I32), plane[8 * i : P : 32, :].bitcast(I32))

        place_bytes = keep.tile([P, S], U8, name="place_bytes")
        nc.vector.tensor_copy(place_bytes[:], scale_table[:].indirect(offs_t[:]))
        place_plane = keep.tile([P, S], U8, name="place_plane", align_bytes=64)
        nc.vector.tensor_copy(place_plane[:].bitcast(I32), place_bytes[:].bitcast(I32))
        close_up_rows(place_plane, nc.scalar)

        w_bf = keep.tile([P, PACK * H], BF16, name="w_bf", align_bytes=64)
        w_dst = w_bf[:].rearrange("p (t m j) -> p m j t", t=PACK, j=PACK)
        w_src = w_raw[:].rearrange("p j (m t) -> p m j t", t=PACK)
        nc.vector.tensor_copy(w_dst[:, :M_SPLIT], w_src[:, :M_SPLIT])
        nc.scalar.copy(w_dst[:, M_SPLIT:], w_src[:, M_SPLIT:])
        w_codes = keep.tile([P, H], U32, name="w_codes", align_bytes=64)
        w_plane = keep.tile([P, H], U8, name="w_plane", align_bytes=64)
        nc.vector.quantize_mx(out=w_codes[:].bitcast(FP8X4), scales=w_plane[:], in_=w_bf[:])

        place_words = keep.tile([P, S], U32, name="place_words", tag="picked_words", align_bytes=64)
        nc.vector.tensor_copy(place_words[:], word_table[:].indirect(offs_t[:]))

        rows = [keep.tile([P, 2 * S], F32, name="rows%d" % t) for t in range(PACK)]

        def product(t, lhs_words, lhs_plane, rhs_words, rhs_plane, dst, factor):
            cols = slice(t * P, (t + 1) * P)
            pieces = 2 if t == 0 else 1
            width = S // pieces
            for h in range(pieces):
                part = slice(h * width, (h + 1) * width)
                bank = psum.tile([P, width], F32, name="bank", tag="bank%d_%d" % (t, h))
                nc.tensor.matmul_mx(
                    out=bank[:], lhsT=lhs_words[:, cols].bitcast(FP8X4), lhsT_scale=lhs_plane[:, cols],
                    rhs=rhs_words[:, part].bitcast(FP8X4), rhs_scale=rhs_plane[:, part], start=True, stop=True,
                )
                if h == 1:
                    nc.scalar.activation(dst[:, part], bank[:], ACT.Copy, scale=factor)
                else:
                    nc.vector.tensor_scalar(dst[:, part], bank[:], factor, None, ALU.mult)

        for t in range(PACK):
            product(t, w_codes, w_plane, place_words, place_plane, rows[t][:, S:], 1.0)

        pair = [[keep.tile([P, W], F32, name="pair%d_%d" % (t, u)) for u in range(2)] for t in range(PACK)]
        sort = [[keep.tile([P, W], F32, name="sort%d_%d" % (t, u)) for u in range(2)] for t in range(PACK)]
        placed = [keep.tile([P, S], F32, name="placed%d" % t) for t in range(PACK)]
        z_bf = [keep.tile([P, S // 2, PACK], BF16, name="z_bf%d" % h, align_bytes=64) for h in range(2)]
        pair_lists = (n1_t, n2_t)

        def fetch(t, u):
            nc.scalar.activation(pair[t][u][:], rows[t][:, S:].indirect(pair_lists[u][:]), ACT.Copy)
            if u == 1:
                nc.vector.tensor_tensor(sort[t][0][:], pair[t][0][:], pair[t][1][:], ALU.max)
                nc.vector.tensor_tensor(sort[t][1][:], pair[t][0][:], pair[t][1][:], ALU.min)

        def put(t, u):
            nc.scalar.activation(placed[t][:].indirect(pair_lists[u][:]), sort[t][u][:], ACT.Copy)
            if u == 1:
                for h in range(2):
                    nc.vector.tensor_scalar(
                        z_bf[h][:, :, t], placed[t][:, h * W : (h + 1) * W], gs_t[:, t : t + 1], None, ALU.mult
                    )

        fetch(0, 0)
        fetch(0, 1)
        fetch(1, 0)
        fetch(1, 1)
        for t in range(2):
            for u in range(2):
                put(t, u)
                fetch(t + 2, u)
        for u in range(2):
            put(2, u)
            put(3, u)

        cand_bytes = keep.tile([P, C], U8, name="cand_bytes")
        nc.vector.tensor_copy(cand_bytes[:], scale_table[:].indirect(cand_t[:]))
        cand_plane = keep.tile([P, C], U8, name="cand_plane", align_bytes=64)
        nc.vector.tensor_copy(
            cand_plane[:].bitcast(I32).rearrange("p (t g) -> p g t", t=PACK),
            cand_bytes[:].bitcast(I32).rearrange("p (g t) -> p g t", t=PACK),
        )
        close_up_rows(cand_plane, nc.sync)
        cand_words = keep.tile([P, C], U32, name="cand_words", tag="picked_words", align_bytes=64)
        nc.vector.tensor_copy(cand_words[:], word_table[:].indirect(cand_t[:]))
        dealt_words = keep.tile([P, C], U32, name="dealt_words", align_bytes=64)
        nc.vector.tensor_copy(
            dealt_words[:].bitcast(I32).rearrange("p (t g a) -> p g t a", t=PACK, a=4),
            cand_words[:].bitcast(I32).rearrange("p (g t a) -> p g t a", t=PACK, a=4),
        )

        z_codes = keep.tile([P, S], U32, name="z_codes", align_bytes=64)
        z_plane = keep.tile([P, S], U8, name="z_plane", align_bytes=64)
        for h in range(2):
            half = slice(h * W, (h + 1) * W)
            nc.vector.quantize_mx(
                out=z_codes[:, half].bitcast(FP8X4), scales=z_plane[:, half],
                in_=z_bf[h][:].rearrange("p j t -> p (j t)"),
            )

        out_rows = out.rearrange("(g t a) j -> t g a j", t=PACK, a=4)
        for t in range(PACK):
            product(t, dealt_words, cand_plane, z_codes, z_plane, rows[t][:, :S], 0.0625)
        for t in range(PACK):
            other = keep.tile([P, S], F32, name="other%d" % t)
            diff = keep.tile([P, S], F32, name="diff%d" % t)
            nc.scalar.activation(other[:], rows[t][:].indirect(n3_t[:]), ACT.Copy)
            nc.vector.tensor_tensor(diff[:], rows[t][:, :S], other[:], ALU.subtract)
            pieces = 2 if t == PACK - 1 else 1
            width = S // pieces
            for h in range(pieces):
                part = slice(h * width, (h + 1) * width)
                gate = keep.tile([P, width], F32, name="gate%d_%d" % (t, h))
                result = keep.tile([P, width], F32, name="result%d_%d" % (t, h))
                offsets = n4_t[:, h * width // 16 : (h + 1) * width // 16]
                nc.scalar.activation(gate[:], rows[t][:].indirect(offsets), ACT.Sigmoid)
                nc.vector.tensor_tensor(result[:], diff[:, part], gate[:], ALU.mult)
                nc.sync.dma_start(out_rows[t][:, :, part], result[:])
